import numpy as np
import ml_dtypes


def mxq(x, axis, fmt="e4m3"):
    dtype, down = {"e4m3": (ml_dtypes.float8_e4m3fn, 7), "e5m2": (ml_dtypes.float8_e5m2, 14)}[fmt]
    v = np.moveaxis(np.asarray(x, np.float32).astype(ml_dtypes.bfloat16).astype(np.float64), axis, -1)
    blocks = v.reshape(v.shape[:-1] + (-1, 32))
    amax = np.abs(blocks).max(-1, keepdims=True)
    byte = np.maximum(np.where(amax > 0, np.frexp(amax)[1] - 1 + 127, 0) - down, 1)
    scale = np.exp2(byte - 127.0)
    codes = (blocks / scale).astype(np.float32).astype(dtype).astype(np.float64)
    return np.moveaxis((codes * scale).reshape(v.shape), -1, axis)


WIDE = False


def mx_kscale(k):
    if not WIDE:
        return np.ones(k)
    levels = np.array([10, -10, 5, -5, 0])
    if k % 512:
        return np.exp2(np.random.permutation(np.resize(levels, k // 32))).repeat(32)
    a = np.empty((k // 512, 16))
    for p in range(k // 512):
        a[p, :8] = np.random.permutation(np.resize(levels, 8))
        for g in range(8):
            far = levels[np.abs(levels - a[p, g]) >= 10]
            a[p, g + 8] = far[np.random.randint(len(far))]
    return np.exp2(a.ravel()).repeat(32)


def f64(x):
    return np.asarray(x).astype(np.float64)


def striped(idx):
    return np.tile(idx.reshape(-1, 16).T, (8, 1)).astype(np.uint16)


def unstriped(offs):
    return offs[:16].T.reshape(-1).astype(np.int64)


def relu2(v):
    return np.maximum(v, 0.0) ** 2


K, T, E, C, N = 512, 1536, 12, 256, 128


def by_expert(wq, xq):
    return np.concatenate([wq[e].T @ xq[:, e * C:(e + 1) * C] for e in range(E)], axis=1)


def setup_inputs():
    n = np.random.standard_normal
    s = mx_kscale(K)[:, None]
    first = np.random.permutation(np.repeat(np.arange(E), T // E))
    second = (first + 1 + np.random.permutation(np.repeat(np.arange(E - 1), -(-T // (E - 1)))[:T])) % E
    while np.bincount(second, minlength=E).max() != T // E:
        load = np.bincount(second, minlength=E); hi, lo = int(load.argmax()), int(load.argmin())
        t = np.flatnonzero((second == hi) & (first != lo))[0]; second[t] = lo
    slot_token = np.empty(E * C, np.int64); pos = np.empty((2, T), np.int64); fill = np.zeros(E, np.int64)
    place = np.stack([np.random.permutation(C) for _ in range(E)])
    for r, deal in enumerate((first, second)):
        for t in np.random.permutation(T):
            e = deal[t]; j = e * C + place[e, fill[e]]; fill[e] += 1; slot_token[j] = t; pos[r, t] = j
    g = np.random.uniform(0.2, 0.8, T)
    return {
        "xT": (n((K, T)) * s).astype(np.float32),
        "w": (n((E + 1, K, N)) / np.sqrt(K) / s[None]).astype(np.float32),
        "b": (0.3 * n((N, E + 1))).astype(np.float32),
        "gate": np.stack([np.tile(g, (N, 1)), np.tile(1.0 - g, (N, 1))]).astype(np.float32),
        "offs": striped(slot_token),
        "pos1": striped(pos[0]),
        "pos2": striped(pos[1]),
    }


def reference(xT, w, b, gate, offs, pos1, pos2):
    idx = unstriped(offs)
    wq = mxq(f64(w), 1, "e4m3")
    xs = mxq(f64(xT), 0, "e4m3")
    ys = relu2((wq[E].T @ xs) + f64(b)[:, E:])
    xq = mxq(f64(xT)[:, idx], 0, "e4m3")
    y = by_expert(wq, xq)
    y = relu2(y + np.repeat(f64(b)[:, :E], C, axis=1))
    return ys + f64(gate[0]) * y[:, unstriped(pos1)] + f64(gate[1]) * y[:, unstriped(pos2)]

@@ -1,0 +1,198 @@
+from contextlib import ExitStack
+
+import concourse.mybir as mybir
+
+F32 = mybir.dt.float32
+BF16 = mybir.dt.bfloat16
+U32 = mybir.dt.uint32
+U16 = mybir.dt.uint16
+U8 = mybir.dt.uint8
+FP8X4 = mybir.dt.float8_e4m3fn_x4
+MULT = mybir.AluOpType.mult
+ADD = mybir.AluOpType.add
+RELU = mybir.ActivationFunctionType.Relu
+SQUARE = mybir.ActivationFunctionType.Square
+
+P = 128
+K, T, E, C, N = 512, 1536, 12, 256, 128
+S = E * C
+TC = 512
+SC = 512
+V_TOKENS = 320
+
+FLOPS = 603979776
+
+
+def tile_moe_shr_lin_relu2_kernel(tc, xT, w, b, gate, offs, pos1, pos2, out):
+    nc = tc.nc
+    with ExitStack() as ctx:
+        lists = ctx.enter_context(tc.tile_pool(name="lists", bufs=1))
+        keep = ctx.enter_context(tc.tile_pool(name="keep", bufs=1))
+        ring = ctx.enter_context(tc.tile_pool(name="ring", bufs=3))
+        psum = ctx.enter_context(tc.psum_pool(name="psum", bufs=6))
+
+        offs_sb = lists.tile([P, S // 16], U16, name="offs_sb")
+        pos1_sb = lists.tile([P, T // 16], U16, name="pos1_sb")
+        pos2_sb = lists.tile([P, T // 16], U16, name="pos2_sb")
+        bias = keep.tile([P, E + 1], F32, name="bias")
+        warm = keep.tile([P, 8], F32, name="warm")
+        nc.vector.memset(warm[:], 0.0)
+        nc.scalar.activation(warm[:], warm[:], RELU)
+
+        x_view = xT.rearrange("(p j) t -> p j t", j=4)
+        w_view = w.rearrange("e (p j) n -> p e j n", j=4)
+        x_raw = [keep.tile([P, 4, TC], F32, name=f"x_raw{i}") for i in range(T // TC)]
+        planes = [keep.tile([P, T, 2], BF16, name=f"plane{u}", align_bytes=64) for u in range(2)]
+
+        def load_x(u, i):
+            nc.sync.dma_start(x_raw[i][:, 2 * u : 2 * u + 2, :], x_view[:, 2 * u : 2 * u + 2, i * TC : (i + 1) * TC])
+
+        for i in range(T // TC):
+            load_x(0, i)
+        nc.sync.dma_start(offs_sb[:], offs)
+        for i in range(T // TC):
+            load_x(1, i)
+        nc.sync.dma_start(bias[:], b)
+        groups = [(2 * g, 2) for g in range(E // 2)] + [(E, 1)]
+        w_raw = []
+        for g, (e0, n_e) in enumerate(groups):
+            raw = keep.tile([P, n_e, 4, N], F32, name=f"w_raw{g}")
+            nc.sync.dma_start(raw[:], w_view[:, e0 : e0 + n_e, :, :])
+            w_raw.append(raw)
+        nc.sync.dma_start(pos1_sb[:], pos1)
+        nc.sync.dma_start(pos2_sb[:], pos2)
+        gates = keep.tile([P, 2, T], F32, name="gates")
+        for h in range(2):
+            nc.sync.dma_start(gates[:, h, :], gate[h])
+
+        def round_pairs(copy, u, i, lo, hi):
+            copy(
+                planes[u][:, i * TC + lo : i * TC + hi, :],
+                x_raw[i][:, 2 * u : 2 * u + 2, lo:hi].rearrange("p e t -> p t e"),
+            )
+
+        for i in range(T // TC):
+            round_pairs(nc.vector.tensor_copy, 0, i, 0, V_TOKENS)
+            round_pairs(nc.scalar.copy, 0, i, V_TOKENS, TC)
+
+        picked = [keep.tile([P, 2, SC, 2], BF16, name=f"picked{c}", align_bytes=64) for c in range(S // SC)]
+
+        def gather(u, c):
+            nc.vector.tensor_copy(
+                picked[c][:, u, :, :].rearrange("p s e -> p (s e)").bitcast(U32),
+                planes[u][:].rearrange("p t e -> p (t e)").bitcast(U32).indirect(offs_sb[:, c * SC // 16 : (c + 1) * SC // 16]),
+            )
+
+        w_codes = keep.tile([P, (E + 1) * N], U32, name="w_codes", align_bytes=64)
+        w_scales = keep.tile([P, (E + 1) * N], U8, name="w_scales", align_bytes=64)
+        w_grouped = [keep.tile([P, n_e * N * 4], BF16, name=f"w_grouped{g}", align_bytes=64) for g, (e0, n_e) in enumerate(groups)]
+
+        def group_w(g):
+            nc.gpsimd.tensor_scalar(
+                w_grouped[g][:].rearrange("p (e n j) -> p e n j", n=N, j=4),
+                w_raw[g][:].rearrange("p e j n -> p e n j"),
+                1.0, 0.0, MULT, ADD,
+            )
+
+        def quantise_w(g):
+            e0, n_e = groups[g]
+            cols = slice(e0 * N, (e0 + n_e) * N)
+            nc.vector.quantize_mx(out=w_codes[:, cols].bitcast(FP8X4), scales=w_scales[:, cols], in_=w_grouped[g][:])
+
+        s_codes = keep.tile([P, S], U32, name="s_codes", align_bytes=64)
+        s_scales = keep.tile([P, S], U8, name="s_scales", align_bytes=64)
+        t_codes = keep.tile([P, T], U32, name="t_codes", align_bytes=64)
+        t_scales = keep.tile([P, T], U8, name="t_scales", align_bytes=64)
+        y = keep.tile([P, S], F32, name="y")
+        ys = keep.tile([P, T], F32, name="ys")
+
+        def product(acc, e, codes, scales, cols):
+            w_cols = slice(e * N, (e + 1) * N)
+            nc.tensor.matmul_mx(
+                out=acc,
+                lhsT=w_codes[:, w_cols].bitcast(FP8X4),
+                lhsT_scale=w_scales[:, w_cols],
+                rhs=codes[:, cols].bitcast(FP8X4),
+                rhs_scale=scales[:, cols],
+                start=True,
+                stop=True,
+            )
+
+        slots = {}
+
+        def interleave(c):
+            slots[c] = ring.tile([P, SC, 4], BF16, name="slots", align_bytes=64)
+            nc.scalar.copy(
+                slots[c][:].rearrange("p s j -> p (s j)").bitcast(F32).rearrange("p (s u) -> p s u", u=2),
+                picked[c][:].rearrange("p u s e -> p (u s e)").bitcast(F32).rearrange("p (u s) -> p s u", u=2),
+            )
+
+        def experts(c):
+            cols = slice(c * SC, (c + 1) * SC)
+            nc.vector.quantize_mx(
+                out=s_codes[:, cols].bitcast(FP8X4), scales=s_scales[:, cols], in_=slots[c][:].rearrange("p s j -> p (s j)")
+            )
+            acc = psum.tile([P, SC], F32, name="acc")
+            r = ring.tile([P, SC], F32, name="r")
+            for h in range(SC // C):
+                e = c * (SC // C) + h
+                part = slice(h * C, (h + 1) * C)
+                product(acc[:, part], e, s_codes, s_scales, slice(e * C, (e + 1) * C))
+                nc.scalar.activation(r[:, part], acc[:, part], RELU, bias=bias[:, e : e + 1])
+            nc.scalar.activation(y[:, cols], r[:], SQUARE)
+
+        xs = [keep.tile([P, TC, 4], BF16, name=f"xs{i}", align_bytes=64) for i in range(T // TC)]
+
+        def group_x(i):
+            nc.gpsimd.tensor_scalar(xs[i][:], x_raw[i][:].rearrange("p j t -> p t j"), 1.0, 0.0, MULT, ADD)
+
+        def shared(i):
+            cols = slice(i * TC, (i + 1) * TC)
+            nc.vector.quantize_mx(
+                out=t_codes[:, cols].bitcast(FP8X4), scales=t_scales[:, cols], in_=xs[i][:].rearrange("p t j -> p (t j)")
+            )
+            acc = psum.tile([P, SC], F32, name="acc")
+            r = ring.tile([P, SC], F32, name="r")
+            product(acc[:], E, t_codes, t_scales, cols)
+            nc.scalar.activation(r[:], acc[:], RELU, bias=bias[:, E : E + 1])
+            nc.gpsimd.tensor_tensor(ys[:, cols], r[:], r[:], MULT)
+
+        for c in range(3):
+            gather(0, c)
+        for i in range(T // TC):
+            round_pairs(nc.scalar.copy, 1, i, 0, TC)
+        for c in range(S // SC):
+            gather(1, c)
+            interleave(c)
+            group_w(c)
+            quantise_w(c)
+            if c + 3 < S // SC:
+                gather(0, c + 3)
+            experts(c)
+        group_w(len(groups) - 1)
+        quantise_w(len(groups) - 1)
+        for i in range(T // TC):
+            group_x(i)
+            shared(i)
+
+        cuts = [0, 512, 1024, 1408, 1536]
+        pieces = list(zip(cuts[:-1], cuts[1:]))
+        first = keep.tile([P, T], F32, name="first")
+        second = keep.tile([P, T], F32, name="second")
+        half = keep.tile([P, T], F32, name="half")
+        total = keep.tile([P, T], F32, name="total")
+
+        def fetch(dst, pos, h, lo, hi):
+            nc.vector.tensor_tensor(dst[:, lo:hi], y[:].indirect(pos[:, lo // 16 : hi // 16]), gates[:, h, lo:hi], MULT)
+
+        def finish(lo, hi):
+            nc.vector.tensor_tensor(total[:, lo:hi], half[:, lo:hi], second[:, lo:hi], ADD)
+            nc.sync.dma_start(out[:, lo:hi], total[:, lo:hi])
+
+        for n, (lo, hi) in enumerate(pieces):
+            fetch(first, pos1_sb, 0, lo, hi)
+            if n > 0:
+                finish(*pieces[n - 1])
+            fetch(second, pos2_sb, 1, lo, hi)
+            nc.vector.tensor_tensor(half[:, lo:hi], first[:, lo:hi], ys[:, lo:hi], ADD)
+        finish(*pieces[-1])

@@ -18,6 +18,8 @@ K, T, E, C, N = 512, 1536, 12, 256, 128
 S = E * C
 TC = 512
 SC = 512
+W_ON_SCALAR = (0, 2)
+X_ON_SCALAR = (0, 1)
 V_TOKENS = 320
 
 FLOPS = 603979776
@@ -42,7 +44,9 @@ def tile_moe_shr_lin_relu2_kernel(tc, xT, w, b, gate, offs, pos1, pos2, out):
         x_view = xT.rearrange("(p j) t -> p j t", j=4)
         w_view = w.rearrange("e (p j) n -> p e j n", j=4)
         x_raw = [keep.tile([P, 4, TC], F32, name=f"x_raw{i}") for i in range(T // TC)]
-        planes = [keep.tile([P, T, 2], BF16, name=f"plane{u}", align_bytes=64) for u in range(2)]
+        both = keep.tile([P, 2, T, 2], BF16, name="both", align_bytes=64)
+        planes = [both[:, u, :, :] for u in range(2)]
+        pairs = both[:].rearrange("p u t e -> p (u t e)").bitcast(F32).rearrange("p (u t) -> p u t", u=2)
 
         def load_x(u, i):
             nc.sync.dma_start(x_raw[i][:, 2 * u : 2 * u + 2, :], x_view[:, 2 * u : 2 * u + 2, i * TC : (i + 1) * TC])
@@ -80,19 +84,21 @@ def tile_moe_shr_lin_relu2_kernel(tc, xT, w, b, gate, offs, pos1, pos2, out):
         def gather(u, c):
             nc.vector.tensor_copy(
                 picked[c][:, u, :, :].rearrange("p s e -> p (s e)").bitcast(U32),
-                planes[u][:].rearrange("p t e -> p (t e)").bitcast(U32).indirect(offs_sb[:, c * SC // 16 : (c + 1) * SC // 16]),
+                planes[u].rearrange("p t e -> p (t e)").bitcast(U32).indirect(offs_sb[:, c * SC // 16 : (c + 1) * SC // 16]),
             )
 
         w_codes = keep.tile([P, (E + 1) * N], U32, name="w_codes", align_bytes=64)
         w_scales = keep.tile([P, (E + 1) * N], U8, name="w_scales", align_bytes=64)
         w_grouped = [keep.tile([P, n_e * N * 4], BF16, name=f"w_grouped{g}", align_bytes=64) for g, (e0, n_e) in enumerate(groups)]
 
-        def group_w(g):
-            nc.gpsimd.tensor_scalar(
-                w_grouped[g][:].rearrange("p (e n j) -> p e n j", n=N, j=4),
-                w_raw[g][:].rearrange("p e j n -> p e n j"),
-                1.0, 0.0, MULT, ADD,
-            )
+        def group_w(e):
+            g, h = divmod(e, 2)
+            dst = w_grouped[g][:, h * N * 4 : (h + 1) * N * 4].rearrange("p (n j) -> p n j", j=4)
+            src = w_raw[g][:, h, :, :].rearrange("p j n -> p n j")
+            if e in W_ON_SCALAR:
+                nc.scalar.copy(dst, src)
+            else:
+                nc.gpsimd.tensor_scalar(dst, src, 1.0, 0.0, MULT, ADD)
 
         def quantise_w(g):
             e0, n_e = groups[g]
@@ -121,7 +127,7 @@ def tile_moe_shr_lin_relu2_kernel(tc, xT, w, b, gate, offs, pos1, pos2, out):
         slots = {}
 
         def interleave(c):
-            slots[c] = ring.tile([P, SC, 4], BF16, name="slots", align_bytes=64)
+            slots[c] = keep.tile([P, SC, 4], BF16, name=f"slots{c}", align_bytes=64)
             nc.scalar.copy(
                 slots[c][:].rearrange("p s j -> p (s j)").bitcast(F32).rearrange("p (s u) -> p s u", u=2),
                 picked[c][:].rearrange("p u s e -> p (u s e)").bitcast(F32).rearrange("p (u s) -> p s u", u=2),
@@ -144,7 +150,9 @@ def tile_moe_shr_lin_relu2_kernel(tc, xT, w, b, gate, offs, pos1, pos2, out):
         xs = [keep.tile([P, TC, 4], BF16, name=f"xs{i}", align_bytes=64) for i in range(T // TC)]
 
         def group_x(i):
-            nc.gpsimd.tensor_scalar(xs[i][:], x_raw[i][:].rearrange("p j t -> p t j"), 1.0, 0.0, MULT, ADD)
+            copy = nc.scalar.copy if i in X_ON_SCALAR else nc.vector.tensor_copy
+            dst = xs[i][:].rearrange("p t j -> p (t j)").bitcast(F32).rearrange("p (t u) -> p t u", u=2)
+            copy(dst, pairs[:, :, i * TC : (i + 1) * TC].rearrange("p u t -> p t u"))
 
         def shared(i):
             cols = slice(i * TC, (i + 1) * TC)
@@ -155,22 +163,25 @@ def tile_moe_shr_lin_relu2_kernel(tc, xT, w, b, gate, offs, pos1, pos2, out):
             r = ring.tile([P, SC], F32, name="r")
             product(acc[:], E, t_codes, t_scales, cols)
             nc.scalar.activation(r[:], acc[:], RELU, bias=bias[:, E : E + 1])
-            nc.gpsimd.tensor_tensor(ys[:, cols], r[:], r[:], MULT)
+            nc.scalar.activation(ys[:, cols], r[:], SQUARE)
 
         for c in range(3):
             gather(0, c)
         for i in range(T // TC):
             round_pairs(nc.scalar.copy, 1, i, 0, TC)
-        for c in range(S // SC):
+        for c in range(3):
+            gather(1, c)
+            gather(0, c + 3)
+            interleave(c)
+        for e in range(E + 1):
+            group_w(e)
+        for c in range(3, 6):
             gather(1, c)
             interleave(c)
-            group_w(c)
+        for c in range(6):
             quantise_w(c)
-            if c + 3 < S // SC:
-                gather(0, c + 3)
             experts(c)
-        group_w(len(groups) - 1)
-        quantise_w(len(groups) - 1)
+        quantise_w(6)
         for i in range(T // TC):
             group_x(i)
             shared(i)

@@ -18,8 +18,8 @@ K, T, E, C, N = 512, 1536, 12, 256, 128
 S = E * C
 TC = 512
 SC = 512
-W_ON_SCALAR = (0, 2)
-X_ON_SCALAR = (0, 1)
+W_ON_SCALAR = tuple(range(E + 1))
+X_ON_SCALAR = ()
 V_TOKENS = 320
 
 FLOPS = 603979776
@@ -79,11 +79,11 @@ def tile_moe_shr_lin_relu2_kernel(tc, xT, w, b, gate, offs, pos1, pos2, out):
             round_pairs(nc.vector.tensor_copy, 0, i, 0, V_TOKENS)
             round_pairs(nc.scalar.copy, 0, i, V_TOKENS, TC)
 
-        picked = [keep.tile([P, 2, SC, 2], BF16, name=f"picked{c}", align_bytes=64) for c in range(S // SC)]
+        slots = [keep.tile([P, SC, 4], BF16, name=f"slots{c}", align_bytes=64) for c in range(S // SC)]
 
         def gather(u, c):
             nc.vector.tensor_copy(
-                picked[c][:, u, :, :].rearrange("p s e -> p (s e)").bitcast(U32),
+                slots[c][:].rearrange("p s j -> p (s j)").bitcast(U32).rearrange("p (s u) -> p s u", u=2)[:, :, u],
                 planes[u].rearrange("p t e -> p (t e)").bitcast(U32).indirect(offs_sb[:, c * SC // 16 : (c + 1) * SC // 16]),
             )
 
@@ -124,15 +124,6 @@ def tile_moe_shr_lin_relu2_kernel(tc, xT, w, b, gate, offs, pos1, pos2, out):
                 stop=True,
             )
 
-        slots = {}
-
-        def interleave(c):
-            slots[c] = keep.tile([P, SC, 4], BF16, name=f"slots{c}", align_bytes=64)
-            nc.scalar.copy(
-                slots[c][:].rearrange("p s j -> p (s j)").bitcast(F32).rearrange("p (s u) -> p s u", u=2),
-                picked[c][:].rearrange("p u s e -> p (u s e)").bitcast(F32).rearrange("p (u s) -> p s u", u=2),
-            )
-
         def experts(c):
             cols = slice(c * SC, (c + 1) * SC)
             nc.vector.quantize_mx(
@@ -169,16 +160,12 @@ def tile_moe_shr_lin_relu2_kernel(tc, xT, w, b, gate, offs, pos1, pos2, out):
             gather(0, c)
         for i in range(T // TC):
             round_pairs(nc.scalar.copy, 1, i, 0, TC)
-        for c in range(3):
-            gather(1, c)
-            gather(0, c + 3)
-            interleave(c)
         for e in range(E + 1):
             group_w(e)
-        for c in range(3, 6):
-            gather(1, c)
-            interleave(c)
         for c in range(6):
+            gather(1, c)
+            if c < 3:
+                gather(0, c + 3)
             quantise_w(c)
             experts(c)
         quantise_w(6)

@@ -14,15 +14,25 @@ RELU = mybir.ActivationFunctionType.Relu
 SQUARE = mybir.ActivationFunctionType.Square
 
 P = 128
-K, T, E, C, N = 512, 1536, 12, 256, 128
+PACK = 4
+K, T, N = P * PACK, 1536, 128
+E, C = 12, 256
 S = E * C
-TC = 512
-SC = 512
-W_ON_SCALAR = tuple(range(E + 1))
-X_ON_SCALAR = ()
-V_TOKENS = 320
+OFFSETS_A_COLUMN = 16
 
-FLOPS = 603979776
+TOKENS = 512
+SLOTS = 2 * C
+CHUNKS = S // SLOTS
+PIECES_OF_X = T // TOKENS
+GROUPS = [range(e, min(e + 2, E + 1)) for e in range(0, E + 1, 2)]
+
+TOKENS_ON_VECTOR = 320
+EARLY_GROUPS = 3
+CHUNKS_ON_SCALAR = 2
+CHUNK_SQUARED_ON_VECTOR = 4
+LAST_STEPS = ((0, 768), (768, 1344), (1344, 1536))
+
+FLOPS = 2 * K * N * (S + T)
 
 
 def tile_moe_shr_lin_relu2_kernel(tc, xT, w, b, gate, offs, pos1, pos2, out):
@@ -33,86 +43,93 @@ def tile_moe_shr_lin_relu2_kernel(tc, xT, w, b, gate, offs, pos1, pos2, out):
         ring = ctx.enter_context(tc.tile_pool(name="ring", bufs=3))
         psum = ctx.enter_context(tc.psum_pool(name="psum", bufs=6))
 
-        offs_sb = lists.tile([P, S // 16], U16, name="offs_sb")
-        pos1_sb = lists.tile([P, T // 16], U16, name="pos1_sb")
-        pos2_sb = lists.tile([P, T // 16], U16, name="pos2_sb")
+        offs_sb = lists.tile([P, S // OFFSETS_A_COLUMN], U16, name="offs_sb")
+        pos1_sb = lists.tile([P, T // OFFSETS_A_COLUMN], U16, name="pos1_sb")
+        pos2_sb = lists.tile([P, T // OFFSETS_A_COLUMN], U16, name="pos2_sb")
+
+        x_raw = [keep.tile([P, PACK, TOKENS], F32, name=f"x_raw{i}") for i in range(PIECES_OF_X)]
+        w_raw = [keep.tile([P, len(group), PACK, N], F32, name=f"w_raw{g}") for g, group in enumerate(GROUPS)]
         bias = keep.tile([P, E + 1], F32, name="bias")
-        warm = keep.tile([P, 8], F32, name="warm")
-        nc.vector.memset(warm[:], 0.0)
-        nc.scalar.activation(warm[:], warm[:], RELU)
+        gates = keep.tile([P, 2, T], F32, name="gates")
+        x_rows = xT.rearrange("(p j) t -> p j t", j=PACK)
+        w_rows = w.rearrange("e (p j) n -> p e j n", j=PACK)
 
-        x_view = xT.rearrange("(p j) t -> p j t", j=4)
-        w_view = w.rearrange("e (p j) n -> p e j n", j=4)
-        x_raw = [keep.tile([P, 4, TC], F32, name=f"x_raw{i}") for i in range(T // TC)]
-        both = keep.tile([P, 2, T, 2], BF16, name="both", align_bytes=64)
-        planes = [both[:, u, :, :] for u in range(2)]
-        pairs = both[:].rearrange("p u t e -> p (u t e)").bitcast(F32).rearrange("p (u t) -> p u t", u=2)
+        def load_x(half):
+            for i in range(PIECES_OF_X):
+                rows = slice(2 * half, 2 * half + 2)
+                nc.sync.dma_start(x_raw[i][:, rows, :], x_rows[:, rows, i * TOKENS : (i + 1) * TOKENS])
 
-        def load_x(u, i):
-            nc.sync.dma_start(x_raw[i][:, 2 * u : 2 * u + 2, :], x_view[:, 2 * u : 2 * u + 2, i * TC : (i + 1) * TC])
+        def load_w(g):
+            group = GROUPS[g]
+            nc.sync.dma_start(w_raw[g][:], w_rows[:, group.start : group.stop, :, :])
 
-        for i in range(T // TC):
-            load_x(0, i)
+        load_x(0)
         nc.sync.dma_start(offs_sb[:], offs)
-        for i in range(T // TC):
-            load_x(1, i)
+        for g in range(EARLY_GROUPS):
+            load_w(g)
+        load_x(1)
         nc.sync.dma_start(bias[:], b)
-        groups = [(2 * g, 2) for g in range(E // 2)] + [(E, 1)]
-        w_raw = []
-        for g, (e0, n_e) in enumerate(groups):
-            raw = keep.tile([P, n_e, 4, N], F32, name=f"w_raw{g}")
-            nc.sync.dma_start(raw[:], w_view[:, e0 : e0 + n_e, :, :])
-            w_raw.append(raw)
+        for g in range(EARLY_GROUPS, len(GROUPS)):
+            load_w(g)
         nc.sync.dma_start(pos1_sb[:], pos1)
         nc.sync.dma_start(pos2_sb[:], pos2)
-        gates = keep.tile([P, 2, T], F32, name="gates")
-        for h in range(2):
-            nc.sync.dma_start(gates[:, h, :], gate[h])
+        for choice in range(2):
+            nc.sync.dma_start(gates[:, choice, :], gate[choice])
 
-        def round_pairs(copy, u, i, lo, hi):
+        x_pairs = keep.tile([P, 2, T, 2], BF16, name="x_pairs", align_bytes=64)
+
+        def words(tile, dtype):
+            return tile[:].rearrange("p a b c -> p (a b c)").bitcast(dtype)
+
+        def round_x(copy, half, i, first, last):
             copy(
-                planes[u][:, i * TC + lo : i * TC + hi, :],
-                x_raw[i][:, 2 * u : 2 * u + 2, lo:hi].rearrange("p e t -> p t e"),
+                x_pairs[:, half, i * TOKENS + first : i * TOKENS + last, :],
+                x_raw[i][:, 2 * half : 2 * half + 2, first:last].rearrange("p e t -> p t e"),
             )
 
-        for i in range(T // TC):
-            round_pairs(nc.vector.tensor_copy, 0, i, 0, V_TOKENS)
-            round_pairs(nc.scalar.copy, 0, i, V_TOKENS, TC)
+        gathered = keep.tile([P, 2, CHUNKS_ON_SCALAR * SLOTS, 2], BF16, name="gathered", align_bytes=64)
+        slots = keep.tile([P, S, 2, 2], BF16, name="slots", align_bytes=64)
+        gathered_by_half = words(gathered, U32).rearrange("p (h s) -> p h s", h=2)
+        slots_by_half = words(slots, U32).rearrange("p (s h) -> p h s", h=2)
 
-        slots = [keep.tile([P, SC, 4], BF16, name=f"slots{c}", align_bytes=64) for c in range(S // SC)]
+        def gather(half, first, last):
+            target = gathered_by_half if first < CHUNKS_ON_SCALAR * SLOTS else slots_by_half
+            columns = slice(first // OFFSETS_A_COLUMN, last // OFFSETS_A_COLUMN)
+            window = words(x_pairs, U32)[:, half * T : (half + 1) * T]
+            nc.vector.tensor_copy(target[:, half, first:last], window.indirect(offs_sb[:, columns]))
 
-        def gather(u, c):
-            nc.vector.tensor_copy(
-                slots[c][:].rearrange("p s j -> p (s j)").bitcast(U32).rearrange("p (s u) -> p s u", u=2)[:, :, u],
-                planes[u].rearrange("p t e -> p (t e)").bitcast(U32).indirect(offs_sb[:, c * SC // 16 : (c + 1) * SC // 16]),
+        def interleave(copy, target, source, cols):
+            copy(
+                words(target, F32).rearrange("p (s h) -> p s h", h=2)[:, cols, :],
+                words(source, F32).rearrange("p (h s) -> p s h", h=2)[:, cols, :],
             )
 
+        w_grouped = [keep.tile([P, len(group), N, PACK], BF16, name=f"w_grouped{g}", align_bytes=64) for g, group in enumerate(GROUPS)]
         w_codes = keep.tile([P, (E + 1) * N], U32, name="w_codes", align_bytes=64)
         w_scales = keep.tile([P, (E + 1) * N], U8, name="w_scales", align_bytes=64)
-        w_grouped = [keep.tile([P, n_e * N * 4], BF16, name=f"w_grouped{g}", align_bytes=64) for g, (e0, n_e) in enumerate(groups)]
+        slot_codes = keep.tile([P, S], U32, name="slot_codes", align_bytes=64)
+        slot_scales = keep.tile([P, S], U8, name="slot_scales", align_bytes=64)
+        token_codes = keep.tile([P, T], U32, name="token_codes", align_bytes=64)
+        token_scales = keep.tile([P, T], U8, name="token_scales", align_bytes=64)
+        tokens = keep.tile([P, T, 2, 2], BF16, name="tokens", align_bytes=64)
 
-        def group_w(e):
-            g, h = divmod(e, 2)
-            dst = w_grouped[g][:, h * N * 4 : (h + 1) * N * 4].rearrange("p (n j) -> p n j", j=4)
-            src = w_raw[g][:, h, :, :].rearrange("p j n -> p n j")
-            if e in W_ON_SCALAR:
-                nc.scalar.copy(dst, src)
-            else:
-                nc.gpsimd.tensor_scalar(dst, src, 1.0, 0.0, MULT, ADD)
+        def quantise(codes, scales, cols, values):
+            nc.vector.quantize_mx(out=codes[:, cols].bitcast(FP8X4), scales=scales[:, cols], in_=values)
+
+        def round_w(e):
+            group, place = divmod(e, 2)
+            nc.gpsimd.tensor_scalar(
+                w_grouped[group][:, place, :, :],
+                w_raw[group][:, place, :, :].rearrange("p j n -> p n j"),
+                1.0, 0.0, MULT, ADD,
+            )
 
         def quantise_w(g):
-            e0, n_e = groups[g]
-            cols = slice(e0 * N, (e0 + n_e) * N)
-            nc.vector.quantize_mx(out=w_codes[:, cols].bitcast(FP8X4), scales=w_scales[:, cols], in_=w_grouped[g][:])
+            group = GROUPS[g]
+            cols = slice(group.start * N, group.stop * N)
+            quantise(w_codes, w_scales, cols, w_grouped[g][:].rearrange("p e n j -> p (e n j)"))
 
-        s_codes = keep.tile([P, S], U32, name="s_codes", align_bytes=64)
-        s_scales = keep.tile([P, S], U8, name="s_scales", align_bytes=64)
-        t_codes = keep.tile([P, T], U32, name="t_codes", align_bytes=64)
-        t_scales = keep.tile([P, T], U8, name="t_scales", align_bytes=64)
-        y = keep.tile([P, S], F32, name="y")
-        ys = keep.tile([P, T], F32, name="ys")
-
-        def product(acc, e, codes, scales, cols):
+        def multiply(acc, e, codes, scales, cols):
             w_cols = slice(e * N, (e + 1) * N)
             nc.tensor.matmul_mx(
                 out=acc,
@@ -124,73 +141,76 @@ def tile_moe_shr_lin_relu2_kernel(tc, xT, w, b, gate, offs, pos1, pos2, out):
                 stop=True,
             )
 
-        def experts(c):
-            cols = slice(c * SC, (c + 1) * SC)
-            nc.vector.quantize_mx(
-                out=s_codes[:, cols].bitcast(FP8X4), scales=s_scales[:, cols], in_=slots[c][:].rearrange("p s j -> p (s j)")
-            )
-            acc = psum.tile([P, SC], F32, name="acc")
-            r = ring.tile([P, SC], F32, name="r")
-            for h in range(SC // C):
-                e = c * (SC // C) + h
-                part = slice(h * C, (h + 1) * C)
-                product(acc[:, part], e, s_codes, s_scales, slice(e * C, (e + 1) * C))
-                nc.scalar.activation(r[:, part], acc[:, part], RELU, bias=bias[:, e : e + 1])
-            nc.scalar.activation(y[:, cols], r[:], SQUARE)
+        y = keep.tile([P, S], F32, name="y")
+        ys = keep.tile([P, T], F32, name="ys")
 
-        xs = [keep.tile([P, TC, 4], BF16, name=f"xs{i}", align_bytes=64) for i in range(T // TC)]
+        def routed_experts(chunk):
+            cols = slice(chunk * SLOTS, (chunk + 1) * SLOTS)
+            quantise(slot_codes, slot_scales, cols, slots[:, cols, :, :].rearrange("p s h e -> p (s h e)"))
+            acc = psum.tile([P, SLOTS], F32, name="acc")
+            positive = ring.tile([P, SLOTS], F32, name="positive")
+            for e in range(2 * chunk, 2 * chunk + 2):
+                part = slice((e - 2 * chunk) * C, (e - 2 * chunk + 1) * C)
+                multiply(acc[:, part], e, slot_codes, slot_scales, slice(e * C, (e + 1) * C))
+                nc.scalar.activation(positive[:, part], acc[:, part], RELU, bias=bias[:, e : e + 1])
+            if chunk == CHUNK_SQUARED_ON_VECTOR:
+                nc.vector.tensor_tensor(y[:, cols], positive[:], positive[:], MULT)
+            else:
+                nc.scalar.activation(y[:, cols], positive[:], SQUARE)
 
-        def group_x(i):
-            copy = nc.scalar.copy if i in X_ON_SCALAR else nc.vector.tensor_copy
-            dst = xs[i][:].rearrange("p t j -> p (t j)").bitcast(F32).rearrange("p (t u) -> p t u", u=2)
-            copy(dst, pairs[:, :, i * TC : (i + 1) * TC].rearrange("p u t -> p t u"))
+        def shared_expert(i):
+            cols = slice(i * TOKENS, (i + 1) * TOKENS)
+            interleave(nc.scalar.copy, tokens, x_pairs, cols)
+            quantise(token_codes, token_scales, cols, tokens[:, cols, :, :].rearrange("p t h e -> p (t h e)"))
+            acc = psum.tile([P, TOKENS], F32, name="acc")
+            positive = ring.tile([P, TOKENS], F32, name="positive")
+            multiply(acc[:], E, token_codes, token_scales, cols)
+            nc.scalar.activation(positive[:], acc[:], RELU, bias=bias[:, E : E + 1])
+            nc.scalar.activation(ys[:, cols], positive[:], SQUARE)
 
-        def shared(i):
-            cols = slice(i * TC, (i + 1) * TC)
-            nc.vector.quantize_mx(
-                out=t_codes[:, cols].bitcast(FP8X4), scales=t_scales[:, cols], in_=xs[i][:].rearrange("p t j -> p (t j)")
-            )
-            acc = psum.tile([P, SC], F32, name="acc")
-            r = ring.tile([P, SC], F32, name="r")
-            product(acc[:], E, t_codes, t_scales, cols)
-            nc.scalar.activation(r[:], acc[:], RELU, bias=bias[:, E : E + 1])
-            nc.scalar.activation(ys[:, cols], r[:], SQUARE)
-
-        for c in range(3):
-            gather(0, c)
-        for i in range(T // TC):
-            round_pairs(nc.scalar.copy, 1, i, 0, TC)
+        for i in range(PIECES_OF_X):
+            round_x(nc.vector.tensor_copy, 0, i, 0, TOKENS_ON_VECTOR)
+            round_x(nc.scalar.copy, 0, i, TOKENS_ON_VECTOR, TOKENS)
+        for first in range(0, S, 2 * SLOTS):
+            gather(0, first, first + 2 * SLOTS)
+        for i in range(PIECES_OF_X):
+            round_x(nc.scalar.copy, 1, i, 0, TOKENS)
         for e in range(E + 1):
-            group_w(e)
-        for c in range(6):
-            gather(1, c)
-            if c < 3:
-                gather(0, c + 3)
-            quantise_w(c)
-            experts(c)
-        quantise_w(6)
-        for i in range(T // TC):
-            group_x(i)
-            shared(i)
+            round_w(e)
+        for g in range(EARLY_GROUPS):
+            quantise_w(g)
 
-        cuts = [0, 512, 1024, 1408, 1536]
-        pieces = list(zip(cuts[:-1], cuts[1:]))
-        first = keep.tile([P, T], F32, name="first")
-        second = keep.tile([P, T], F32, name="second")
-        half = keep.tile([P, T], F32, name="half")
+        for chunk in range(CHUNKS + 1):
+            if chunk < CHUNKS:
+                gather(1, chunk * SLOTS, (chunk + 1) * SLOTS)
+            if chunk < CHUNKS_ON_SCALAR:
+                interleave(nc.scalar.copy, slots, gathered, slice(chunk * SLOTS, (chunk + 1) * SLOTS))
+            if chunk > 0:
+                if chunk - 1 >= EARLY_GROUPS:
+                    quantise_w(chunk - 1)
+                routed_experts(chunk - 1)
+        quantise_w(len(GROUPS) - 1)
+        for i in range(PIECES_OF_X):
+            shared_expert(i)
+
+        first_choice = keep.tile([P, T], F32, name="first_choice")
+        second_choice = keep.tile([P, T], F32, name="second_choice")
+        partial = keep.tile([P, T], F32, name="partial")
         total = keep.tile([P, T], F32, name="total")
 
-        def fetch(dst, pos, h, lo, hi):
-            nc.vector.tensor_tensor(dst[:, lo:hi], y[:].indirect(pos[:, lo // 16 : hi // 16]), gates[:, h, lo:hi], MULT)
+        def fetch(target, pos, choice, cols):
+            columns = slice(cols.start // OFFSETS_A_COLUMN, cols.stop // OFFSETS_A_COLUMN)
+            nc.vector.tensor_tensor(target[:, cols], y[:].indirect(pos[:, columns]), gates[:, choice, cols], MULT)
 
-        def finish(lo, hi):
-            nc.vector.tensor_tensor(total[:, lo:hi], half[:, lo:hi], second[:, lo:hi], ADD)
-            nc.sync.dma_start(out[:, lo:hi], total[:, lo:hi])
+        def finish(cols):
+            nc.vector.tensor_tensor(total[:, cols], partial[:, cols], second_choice[:, cols], ADD)
+            nc.sync.dma_start(out[:, cols], total[:, cols])
 
-        for n, (lo, hi) in enumerate(pieces):
-            fetch(first, pos1_sb, 0, lo, hi)
+        steps = [slice(first, last) for first, last in LAST_STEPS]
+        for n, cols in enumerate(steps):
+            fetch(first_choice, pos1_sb, 0, cols)
             if n > 0:
-                finish(*pieces[n - 1])
-            fetch(second, pos2_sb, 1, lo, hi)
-            nc.vector.tensor_tensor(half[:, lo:hi], first[:, lo:hi], ys[:, lo:hi], ADD)
-        finish(*pieces[-1])
+                finish(steps[n - 1])
+            fetch(second_choice, pos2_sb, 1, cols)
+            nc.vector.tensor_tensor(partial[:, cols], first_choice[:, cols], ys[:, cols], ADD)
+        finish(steps[-1])

from contextlib import ExitStack

import concourse.mybir as mybir

F32 = mybir.dt.float32
BF16 = mybir.dt.bfloat16
U32 = mybir.dt.uint32
U16 = mybir.dt.uint16
U8 = mybir.dt.uint8
FP8X4 = mybir.dt.float8_e4m3fn_x4
MULT = mybir.AluOpType.mult
ADD = mybir.AluOpType.add
RELU = mybir.ActivationFunctionType.Relu
SQUARE = mybir.ActivationFunctionType.Square

P = 128
PACK = 4
K, T, N = P * PACK, 1536, 128
E, C = 12, 256
S = E * C
OFFSETS_A_COLUMN = 16

TOKENS = 512
SLOTS = 2 * C
CHUNKS = S // SLOTS
PIECES_OF_X = T // TOKENS
GROUPS = [range(e, min(e + 2, E + 1)) for e in range(0, E + 1, 2)]

TOKENS_ON_VECTOR = 320
EARLY_GROUPS = 3
CHUNKS_ON_SCALAR = 2
CHUNK_SQUARED_ON_VECTOR = 4
LAST_STEPS = ((0, 768), (768, 1344), (1344, 1536))

FLOPS = 2 * K * N * (S + T)


def tile_moe_shr_lin_relu2_kernel(tc, xT, w, b, gate, offs, pos1, pos2, out):
    nc = tc.nc
    with ExitStack() as ctx:
        lists = ctx.enter_context(tc.tile_pool(name="lists", bufs=1))
        keep = ctx.enter_context(tc.tile_pool(name="keep", bufs=1))
        ring = ctx.enter_context(tc.tile_pool(name="ring", bufs=3))
        psum = ctx.enter_context(tc.psum_pool(name="psum", bufs=6))

        offs_sb = lists.tile([P, S // OFFSETS_A_COLUMN], U16, name="offs_sb")
        pos1_sb = lists.tile([P, T // OFFSETS_A_COLUMN], U16, name="pos1_sb")
        pos2_sb = lists.tile([P, T // OFFSETS_A_COLUMN], U16, name="pos2_sb")

        x_raw = [keep.tile([P, PACK, TOKENS], F32, name=f"x_raw{i}") for i in range(PIECES_OF_X)]
        w_raw = [keep.tile([P, len(group), PACK, N], F32, name=f"w_raw{g}") for g, group in enumerate(GROUPS)]
        bias = keep.tile([P, E + 1], F32, name="bias")
        gates = keep.tile([P, 2, T], F32, name="gates")
        x_rows = xT.rearrange("(p j) t -> p j t", j=PACK)
        w_rows = w.rearrange("e (p j) n -> p e j n", j=PACK)

        def load_x(half):
            for i in range(PIECES_OF_X):
                rows = slice(2 * half, 2 * half + 2)
                nc.sync.dma_start(x_raw[i][:, rows, :], x_rows[:, rows, i * TOKENS : (i + 1) * TOKENS])

        def load_w(g):
            group = GROUPS[g]
            nc.sync.dma_start(w_raw[g][:], w_rows[:, group.start : group.stop, :, :])

        load_x(0)
        nc.sync.dma_start(offs_sb[:], offs)
        for g in range(EARLY_GROUPS):
            load_w(g)
        load_x(1)
        nc.sync.dma_start(bias[:], b)
        for g in range(EARLY_GROUPS, len(GROUPS)):
            load_w(g)
        nc.sync.dma_start(pos1_sb[:], pos1)
        nc.sync.dma_start(pos2_sb[:], pos2)
        for choice in range(2):
            nc.sync.dma_start(gates[:, choice, :], gate[choice])

        x_pairs = keep.tile([P, 2, T, 2], BF16, name="x_pairs", align_bytes=64)

        def words(tile, dtype):
            return tile[:].rearrange("p a b c -> p (a b c)").bitcast(dtype)

        def round_x(copy, half, i, first, last):
            copy(
                x_pairs[:, half, i * TOKENS + first : i * TOKENS + last, :],
                x_raw[i][:, 2 * half : 2 * half + 2, first:last].rearrange("p e t -> p t e"),
            )

        gathered = keep.tile([P, 2, CHUNKS_ON_SCALAR * SLOTS, 2], BF16, name="gathered", align_bytes=64)
        slots = keep.tile([P, S, 2, 2], BF16, name="slots", align_bytes=64)
        gathered_by_half = words(gathered, U32).rearrange("p (h s) -> p h s", h=2)
        slots_by_half = words(slots, U32).rearrange("p (s h) -> p h s", h=2)

        def gather(half, first, last):
            target = gathered_by_half if first < CHUNKS_ON_SCALAR * SLOTS else slots_by_half
            columns = slice(first // OFFSETS_A_COLUMN, last // OFFSETS_A_COLUMN)
            window = words(x_pairs, U32)[:, half * T : (half + 1) * T]
            nc.vector.tensor_copy(target[:, half, first:last], window.indirect(offs_sb[:, columns]))

        def interleave(copy, target, source, cols):
            copy(
                words(target, F32).rearrange("p (s h) -> p s h", h=2)[:, cols, :],
                words(source, F32).rearrange("p (h s) -> p s h", h=2)[:, cols, :],
            )

        w_grouped = [keep.tile([P, len(group), N, PACK], BF16, name=f"w_grouped{g}", align_bytes=64) for g, group in enumerate(GROUPS)]
        w_codes = keep.tile([P, (E + 1) * N], U32, name="w_codes", align_bytes=64)
        w_scales = keep.tile([P, (E + 1) * N], U8, name="w_scales", align_bytes=64)
        slot_codes = keep.tile([P, S], U32, name="slot_codes", align_bytes=64)
        slot_scales = keep.tile([P, S], U8, name="slot_scales", align_bytes=64)
        token_codes = keep.tile([P, T], U32, name="token_codes", align_bytes=64)
        token_scales = keep.tile([P, T], U8, name="token_scales", align_bytes=64)
        tokens = keep.tile([P, T, 2, 2], BF16, name="tokens", align_bytes=64)

        def quantise(codes, scales, cols, values):
            nc.vector.quantize_mx(out=codes[:, cols].bitcast(FP8X4), scales=scales[:, cols], in_=values)

        def round_w(e):
            group, place = divmod(e, 2)
            nc.gpsimd.tensor_scalar(
                w_grouped[group][:, place, :, :],
                w_raw[group][:, place, :, :].rearrange("p j n -> p n j"),
                1.0, 0.0, MULT, ADD,
            )

        def quantise_w(g):
            group = GROUPS[g]
            cols = slice(group.start * N, group.stop * N)
            quantise(w_codes, w_scales, cols, w_grouped[g][:].rearrange("p e n j -> p (e n j)"))

        def multiply(acc, e, codes, scales, cols):
            w_cols = slice(e * N, (e + 1) * N)
            nc.tensor.matmul_mx(
                out=acc,
                lhsT=w_codes[:, w_cols].bitcast(FP8X4),
                lhsT_scale=w_scales[:, w_cols],
                rhs=codes[:, cols].bitcast(FP8X4),
                rhs_scale=scales[:, cols],
                start=True,
                stop=True,
            )

        y = keep.tile([P, S], F32, name="y")
        ys = keep.tile([P, T], F32, name="ys")

        def routed_experts(chunk):
            cols = slice(chunk * SLOTS, (chunk + 1) * SLOTS)
            quantise(slot_codes, slot_scales, cols, slots[:, cols, :, :].rearrange("p s h e -> p (s h e)"))
            acc = psum.tile([P, SLOTS], F32, name="acc")
            positive = ring.tile([P, SLOTS], F32, name="positive")
            for e in range(2 * chunk, 2 * chunk + 2):
                part = slice((e - 2 * chunk) * C, (e - 2 * chunk + 1) * C)
                multiply(acc[:, part], e, slot_codes, slot_scales, slice(e * C, (e + 1) * C))
                nc.scalar.activation(positive[:, part], acc[:, part], RELU, bias=bias[:, e : e + 1])
            if chunk == CHUNK_SQUARED_ON_VECTOR:
                nc.vector.tensor_tensor(y[:, cols], positive[:], positive[:], MULT)
            else:
                nc.scalar.activation(y[:, cols], positive[:], SQUARE)

        def shared_expert(i):
            cols = slice(i * TOKENS, (i + 1) * TOKENS)
            interleave(nc.scalar.copy, tokens, x_pairs, cols)
            quantise(token_codes, token_scales, cols, tokens[:, cols, :, :].rearrange("p t h e -> p (t h e)"))
            acc = psum.tile([P, TOKENS], F32, name="acc")
            positive = ring.tile([P, TOKENS], F32, name="positive")
            multiply(acc[:], E, token_codes, token_scales, cols)
            nc.scalar.activation(positive[:], acc[:], RELU, bias=bias[:, E : E + 1])
            nc.scalar.activation(ys[:, cols], positive[:], SQUARE)

        for i in range(PIECES_OF_X):
            round_x(nc.vector.tensor_copy, 0, i, 0, TOKENS_ON_VECTOR)
            round_x(nc.scalar.copy, 0, i, TOKENS_ON_VECTOR, TOKENS)
        for first in range(0, S, 2 * SLOTS):
            gather(0, first, first + 2 * SLOTS)
        for i in range(PIECES_OF_X):
            round_x(nc.scalar.copy, 1, i, 0, TOKENS)
        for e in range(E + 1):
            round_w(e)
        for g in range(EARLY_GROUPS):
            quantise_w(g)

        for chunk in range(CHUNKS + 1):
            if chunk < CHUNKS:
                gather(1, chunk * SLOTS, (chunk + 1) * SLOTS)
            if chunk < CHUNKS_ON_SCALAR:
                interleave(nc.scalar.copy, slots, gathered, slice(chunk * SLOTS, (chunk + 1) * SLOTS))
            if chunk > 0:
                if chunk - 1 >= EARLY_GROUPS:
                    quantise_w(chunk - 1)
                routed_experts(chunk - 1)
        quantise_w(len(GROUPS) - 1)
        for i in range(PIECES_OF_X):
            shared_expert(i)

        first_choice = keep.tile([P, T], F32, name="first_choice")
        second_choice = keep.tile([P, T], F32, name="second_choice")
        partial = keep.tile([P, T], F32, name="partial")
        total = keep.tile([P, T], F32, name="total")

        def fetch(target, pos, choice, cols):
            columns = slice(cols.start // OFFSETS_A_COLUMN, cols.stop // OFFSETS_A_COLUMN)
            nc.vector.tensor_tensor(target[:, cols], y[:].indirect(pos[:, columns]), gates[:, choice, cols], MULT)

        def finish(cols):
            nc.vector.tensor_tensor(total[:, cols], partial[:, cols], second_choice[:, cols], ADD)
            nc.sync.dma_start(out[:, cols], total[:, cols])

        steps = [slice(first, last) for first, last in LAST_STEPS]
        for n, cols in enumerate(steps):
            fetch(first_choice, pos1_sb, 0, cols)
            if n > 0:
                finish(steps[n - 1])
            fetch(second_choice, pos2_sb, 1, cols)
            nc.vector.tensor_tensor(partial[:, cols], first_choice[:, cols], ys[:, cols], ADD)
        finish(steps[-1])
